import numpy as np
import ml_dtypes


def mxq(x, axis, fmt="e4m3"):
    dtype, down = {"e4m3": (ml_dtypes.float8_e4m3fn, 7), "e5m2": (ml_dtypes.float8_e5m2, 14)}[fmt]
    v = np.moveaxis(np.asarray(x, np.float32).astype(ml_dtypes.bfloat16).astype(np.float64), axis, -1)
    blocks = v.reshape(v.shape[:-1] + (-1, 32))
    amax = np.abs(blocks).max(-1, keepdims=True)
    byte = np.maximum(np.where(amax > 0, np.frexp(amax)[1] - 1 + 127, 0) - down, 1)
    scale = np.exp2(byte - 127.0)
    codes = (blocks / scale).astype(np.float32).astype(dtype).astype(np.float64)
    return np.moveaxis((codes * scale).reshape(v.shape), -1, axis)


WIDE = False


def mx_kscale(k):
    if not WIDE:
        return np.ones(k)
    levels = np.array([10, -10, 5, -5, 0])
    if k % 512:
        return np.exp2(np.random.permutation(np.resize(levels, k // 32))).repeat(32)
    a = np.empty((k // 512, 16))
    for p in range(k // 512):
        a[p, :8] = np.random.permutation(np.resize(levels, 8))
        for g in range(8):
            far = levels[np.abs(levels - a[p, g]) >= 10]
            a[p, g + 8] = far[np.random.randint(len(far))]
    return np.exp2(a.ravel()).repeat(32)


def f64(x):
    return np.asarray(x).astype(np.float64)


def striped(idx):
    return np.tile(idx.reshape(-1, 16).T, (8, 1)).astype(np.uint16)


def unstriped(offs):
    return offs[:16].T.reshape(-1).astype(np.int64)


E2M1 = np.array([0.0, 0.5, 1.0, 1.5, 2.0, 3.0, 4.0, 6.0, -0.0, -0.5, -1.0, -1.5, -2.0, -3.0, -4.0, -6.0])


def pack_weight(w, fmt):
    k, n = w.shape
    w = f64(np.asarray(w, np.float32).astype(ml_dtypes.bfloat16)).reshape(k // 32, 32, n)
    amax = np.abs(w).max(1)
    if fmt == "e4m3":
        byte = np.frexp(amax)[1] - 1 + 127 - 7
    else:
        mant, ex = np.frexp(amax / 6.0)
        byte = np.where(mant > 0.5, ex, ex - 1) + 127
    byte = np.clip(np.where(amax > 0, byte, 1), 1, 254)
    scaled = (w * np.exp2(127.0 - byte)[:, None, :]).reshape(k, n).astype(np.float32)
    by_word = np.ascontiguousarray(scaled.reshape(k // 512, 128, 4, n).transpose(0, 1, 3, 2))
    if fmt == "e4m3":
        words = by_word.astype(ml_dtypes.float8_e4m3fn).view(np.uint8)
    else:
        c = by_word.astype(ml_dtypes.float4_e2m1fn).view(np.uint8) & 0xF
        words = (c[..., 0::2] | (c[..., 1::2] << 4)).reshape(k // 512, 128, 2 * n)
    return np.ascontiguousarray(words), np.ascontiguousarray(byte.astype(np.uint8).reshape(k // 512, 16, n))


def unpack_weight(words, scales, fmt):
    g, _, n = scales.shape
    words = np.ascontiguousarray(words).reshape(g, 128, n, -1)
    if fmt == "e4m3":
        vals = words.view(ml_dtypes.float8_e4m3fn).astype(np.float64)
    else:
        nib = np.empty((g, 128, n, 4), np.uint8)
        nib[..., 0::2] = words & 0xF
        nib[..., 1::2] = words >> 4
        vals = E2M1[nib]
    vals = vals * np.repeat(np.exp2(scales.astype(np.float64) - 127.0), 8, axis=1)[..., None]
    return vals.transpose(0, 1, 3, 2).reshape(g * 512, n)


def gelu(v):
    return 0.5 * v * (1.0 + np.tanh(np.sqrt(2.0 / np.pi) * (v + 0.044715 * v**3)))


def bf(x):
    return np.asarray(x, np.float32).astype(ml_dtypes.bfloat16)


def planes(Y):
    n, m = Y.shape
    b = f64(bf(Y)).reshape(n // 32, 32, m)
    amax = np.abs(b).max(1)
    byte = np.clip(np.where(amax > 0, np.frexp(amax)[1] - 1 + 127 - 7, 1), 1, 254)
    codes = (b * np.exp2(127.0 - byte)[:, None, :]).reshape(n, m).astype(np.float32).astype(ml_dtypes.float8_e4m3fn).view(np.uint8)
    words = codes.reshape(n // 512, 128, 4, m).transpose(0, 1, 3, 2)
    return np.ascontiguousarray(words), np.ascontiguousarray(byte.astype(np.uint8).reshape(n // 512, 16, m))


K, T, S, H, N = 512, 4096, 1024, 1536, 512

def setup_inputs():
    n = np.random.standard_normal
    s = mx_kscale(K)[:, None]
    u = mx_kscale(H)[:, None]
    tab_words, tab_scales = pack_weight(n((K, T)) * s, "e2m1")
    offs = striped(np.random.permutation(T)[:S])
    offs2 = striped(np.random.permutation(T)[:S])
    w1 = (n((K, H)) / np.sqrt(K) / s).astype(np.float32)
    w8_words, w8_scales = pack_weight(n((K, H)) / np.sqrt(K) / s, "e4m3")
    traffic = (np.exp(0.5 * n((H, S))) * u).astype(np.float32)
    w4_words, w4_scales = pack_weight(n((H, N)) / np.sqrt(H) * np.exp(0.8 * n((1, N))) / u, "e2m1")
    return {"tab_words": tab_words, "tab_scales": tab_scales, "offs": offs, "offs2": offs2,
            "w1": w1, "w8_words": w8_words, "w8_scales": w8_scales, "traffic": traffic,
            "w4_words": w4_words, "w4_scales": w4_scales}

def reference(tab_words, tab_scales, offs, offs2, w1, w8_words, w8_scales, traffic, w4_words, w4_scales):
    TW = unpack_weight(tab_words, tab_scales, "e2m1")
    v = TW[:, unstriped(offs)]
    v2 = TW[:, unstriped(offs2)]
    a = mxq(f64(w1), 0, "e4m3").T @ v
    b = unpack_weight(w8_words, w8_scales, "e4m3").T @ v2
    z = (np.log1p(np.square(a)) - np.log1p(np.square(b))) * f64(traffic)
    zq = mxq(z, 0, "e4m3")
    y = unpack_weight(w4_words, w4_scales, "e2m1").T @ zq
    words, scales = planes(y)
    return y, words, scales

@@ -1,0 +1,290 @@
+from contextlib import ExitStack
+
+import concourse.mybir as mybir
+from concourse.masks import make_identity
+
+K, T, S, H, N = 512, 4096, 1024, 1536, 512
+FLOPS = 2 * K * H * S * 2 + 2 * H * N * S
+
+F32 = mybir.dt.float32
+BF16 = mybir.dt.bfloat16
+I32 = mybir.dt.int32
+U16 = mybir.dt.uint16
+U8 = mybir.dt.uint8
+FP8X4 = mybir.dt.float8_e4m3fn_x4
+FP4X4 = mybir.dt.float4_e2m1fn_x4
+ACT = mybir.ActivationFunctionType
+ALU = mybir.AluOpType
+
+P = 128
+PACK = 4
+PASS = P * PACK
+GROUPS = H // PASS
+HALF = 512
+HALVES = S // HALF
+BLOCKS = S // P
+BLOCKS_PER_HALF = HALF // P
+LEAD = 4
+WALK = 2
+
+
+def tile_list_codeshare_alliance_contrast_kernel(
+    tc, tab_words, tab_scales, offs, offs2, w1, w8_words, w8_scales, traffic, w4_words, w4_scales, out_0, out_1, out_2
+):
+    nc = tc.nc
+    with ExitStack() as ctx:
+        lists = ctx.enter_context(tc.tile_pool(name="lists", bufs=1))
+        keep = ctx.enter_context(tc.tile_pool(name="keep", bufs=1))
+        ring = ctx.enter_context(tc.tile_pool(name="ring", bufs=1))
+        psum = ctx.enter_context(tc.psum_pool(name="psum", bufs=1))
+
+        list_a = lists.tile([P, S // 16], U16, name="list_a")
+        list_b = lists.tile([P, S // 16], U16, name="list_b")
+        tab_w = keep.tile([P, T], U16, name="tab_w", align_bytes=64)
+        tab_s = keep.tile([P, T], U8, name="tab_s", align_bytes=64)
+        w8_first = keep.tile([P, PASS], I32, name="w8_first", align_bytes=64)
+        w8_s = keep.tile([P, H], U8, name="w8_s", align_bytes=64)
+        w4_w = keep.tile([P, GROUPS, PACK, P], U16, name="w4_w", align_bytes=64)
+        w4_s = keep.tile([P, GROUPS, PACK, P], U8, name="w4_s", align_bytes=64)
+        w1_w = [keep.tile([P, PASS], I32, name="w1_w%d" % g, align_bytes=64) for g in range(GROUPS)]
+        w1_s = [keep.tile([P, PASS], U8, name="w1_s%d" % g, align_bytes=64) for g in range(GROUPS)]
+        picked_w = {
+            (side, h): keep.tile([P, HALF], U16, name="picked_w%s%d" % (side, h), align_bytes=64) for side in "ab" for h in range(HALVES)
+        }
+        picked_s = {
+            (side, h): keep.tile([P, HALF], U8, name="picked_s%s%d" % (side, h), align_bytes=64) for side in "ab" for h in range(HALVES)
+        }
+        identity = keep.tile([P, P], F32, name="identity")
+        y_w = keep.tile([P, S], I32, name="y_w", align_bytes=64)
+        y_s = keep.tile([P, S], U8, name="y_s", align_bytes=64)
+        warm_in = keep.tile([P, 1], F32, name="warm_in", tag="floats", align_bytes=64)
+        warm_out = keep.tile([P, 1], F32, name="warm_out", tag="words", align_bytes=64)
+
+        nc.vector.memset(warm_in[:], 1.0)
+        nc.vector.memset(tab_s[:].bitcast(I32), 0)
+        nc.vector.memset(w8_s[:].bitcast(I32), 0)
+        nc.scalar.activation(out=warm_out[:], in_=warm_in[:], func=ACT.Ln, bias=1.0)
+        piece = PACK * PASS
+        floats = keep.tile([P, (GROUPS + GROUPS * HALVES) * piece], F32, name="floats", tag="floats", align_bytes=64)
+        pieces = [floats[:, i * piece : (i + 1) * piece].rearrange("p (t c) -> p t c", t=PACK) for i in range(GROUPS + GROUPS * HALVES)]
+        w1_raw = pieces[:GROUPS]
+        weights = {(g, h): pieces[GROUPS + h * GROUPS + g] for g in range(GROUPS) for h in range(HALVES)}
+        words = keep.tile([P, H - PASS + GROUPS * N // 2 + GROUPS * N // 4], I32, name="words", tag="words", align_bytes=64)
+        w8_w = [w8_first[:], words[:, 0:PASS], words[:, PASS : 2 * PASS]]
+        w4_raw_w = words[:, H - PASS : H - PASS + GROUPS * N // 2].rearrange("p (g c) -> p g c", g=GROUPS)
+        w4_raw_s = words[:, H - PASS + GROUPS * N // 2 :]
+        w8_rows = w8_words[0].rearrange("p c i -> p (c i)").bitcast(I32)
+        nc.sync.dma_start(list_b[:], offs2)
+        nc.sync.dma_start(list_a[:], offs)
+        nc.sync.dma_start(out=tab_w[:].bitcast(I32), in_=tab_words[0].bitcast(I32))
+        nc.sync.dma_start(out=w8_first[:], in_=w8_rows[:, 0:PASS])
+        for q in range(4):
+            nc.sync.dma_start(out=tab_s[32 * q : 32 * q + 4, :].bitcast(I32), in_=tab_scales[0, 4 * q : 4 * q + 4, :].bitcast(I32))
+        for q in range(4):
+            nc.sync.dma_start(out=w8_s[32 * q : 32 * q + 4, :].bitcast(I32), in_=w8_scales[0, 4 * q : 4 * q + 4, :].bitcast(I32))
+
+
+        def load_w1(g):
+            nc.sync.dma_start(out=w1_raw[g], in_=w1[:, g * PASS : (g + 1) * PASS].rearrange("(p t) c -> p t c", t=PACK))
+
+        def load_traffic(g, h):
+            rows = traffic[g * PASS : (g + 1) * PASS, h * HALF : (h + 1) * HALF]
+            nc.sync.dma_start(out=weights[g, h], in_=rows.rearrange("(p t) j -> p t j", t=PACK))
+
+        make_identity(nc, identity[:])
+        load_w1(0)
+        nc.sync.dma_start(out=words[:, 0 : H - PASS], in_=w8_rows[:, PASS:H])
+        load_traffic(0, 0)
+        load_w1(1)
+        nc.sync.dma_start(out=w4_raw_w, in_=w4_words.rearrange("g p b -> p g b").bitcast(I32))
+        nc.gpsimd.memset(w4_raw_s, 0)
+        for q in range(4):
+            nc.sync.dma_start(
+                out=w4_raw_s[32 * q : 32 * q + 4, :].rearrange("q (g c) -> q g c", g=GROUPS),
+                in_=w4_scales[:, 4 * q : 4 * q + 4, :].rearrange("g q c -> q g c").bitcast(I32),
+            )
+        load_traffic(1, 0)
+        load_w1(2)
+        load_traffic(2, 0)
+        for g in range(GROUPS):
+            load_traffic(g, 1)
+
+
+        def gather(side, h):
+            entries = (list_a if side == "a" else list_b)[:, h * HALF // 16 : (h + 1) * HALF // 16]
+            nc.vector.tensor_copy(picked_w[side, h][:], tab_w[:].indirect(entries))
+            nc.vector.tensor_copy(picked_s[side, h][:], tab_s[:].indirect(entries))
+
+        w1_bf = {}
+
+        def round_w1(g):
+            w1_bf[g] = ring.tile([P, PASS, PACK], BF16, name="w1_bf", bufs=2, align_bytes=64)
+            nc.vector.tensor_copy(
+                out=w1_bf[g][:].rearrange("p (c i) t -> p c t i", i=4),
+                in_=w1_raw[g].rearrange("p t (c i) -> p c t i", i=4),
+            )
+
+        def quantize_w1(g):
+            nc.vector.quantize_mx(out=w1_w[g][:].bitcast(FP8X4), scales=w1_s[g][:], in_=w1_bf[g][:].rearrange("p c t -> p (c t)"))
+
+        def deal_w4():
+            for g in range(GROUPS):
+                nc.vector.tensor_copy(out=w4_w[:, g, :, :], in_=w4_raw_w[:, g, :].bitcast(U16).rearrange("p (m t) -> p t m", t=PACK))
+            nc.vector.tensor_copy(out=w4_s[:], in_=w4_raw_s.bitcast(U8).rearrange("p (g m t) -> p g t m", g=GROUPS, t=PACK))
+
+        units = [(b, g) for g in range(GROUPS) for b in range(BLOCKS_PER_HALF)]
+        units = units + [(b, g) for b in range(BLOCKS_PER_HALF, BLOCKS) for g in range(GROUPS)]
+        tasks = [("b", u) for u in range(LEAD)]
+        ahead = LEAD
+        for u in range(len(units)):
+            tasks.append(("a", u))
+            if ahead < len(units) and u not in (7, 14):
+                tasks.append(("b", ahead))
+                ahead = ahead + 1
+        steps = [tasks[i : i + 2] for i in range(0, len(tasks) - 2, 2)] + [tasks[-2:-1], tasks[-1:]]
+
+        squares, logs_a, logs_b, z_bf, z_w, z_s, y_bank, y_f32, y_bf = {}, {}, {}, {}, {}, {}, {}, {}, {}
+
+        def first_product(side, u, target):
+            b, g = units[u]
+            h, cols = b // BLOCKS_PER_HALF, slice((b % BLOCKS_PER_HALF) * P, (b % BLOCKS_PER_HALF + 1) * P)
+            bank = psum.tile([P, PASS], F32, name="first", bufs=4)
+            nc.tensor.matmul_mx(
+                out=bank[:],
+                lhsT=picked_w[side, h][:, cols].bitcast(FP4X4),
+                lhsT_scale=picked_s[side, h][:, cols],
+                rhs=(w1_w[g][:] if side == "a" else w8_w[g]).bitcast(FP8X4),
+                rhs_scale=w1_s[g][:] if side == "a" else w8_s[:, g * PASS : (g + 1) * PASS],
+                start=True,
+                stop=True,
+            )
+            nc.scalar.activation(
+                out=target.rearrange("p (t m) -> p t m", t=PACK), in_=bank[:].rearrange("p (m t) -> p t m", t=PACK), func=ACT.Square
+            )
+
+        def square_step(s):
+            squares[s] = ring.tile([P, 2, PASS], F32, name="squares", bufs=3)
+            for k, (side, u) in enumerate(steps[s]):
+                first_product(side, u, squares[s][:, k, :])
+
+        def log_step(s):
+            logs = ring.tile([P, 2, PASS], F32, name="logs", bufs=4)
+            nc.scalar.activation(out=logs[:, 0 : len(steps[s]), :], in_=squares[s][:, 0 : len(steps[s]), :], func=ACT.Ln, bias=1.0)
+            for k, (side, u) in enumerate(steps[s]):
+                if side == "a":
+                    logs_a[u] = logs[:, k, :]
+                else:
+                    negated = ring.tile([P, PASS], F32, name="negated", bufs=LEAD + 3)
+                    nc.gpsimd.tensor_scalar(negated[:], logs[:, k, :], -1.0, 0.0, ALU.mult, ALU.add)
+                    logs_b[u] = negated[:]
+
+        def contrast(u):
+            b, g = units[u]
+            h, cols = b // BLOCKS_PER_HALF, slice((b % BLOCKS_PER_HALF) * P, (b % BLOCKS_PER_HALF + 1) * P)
+            bank = psum.tile([P, PACK, P], F32, name="difference", bufs=2)
+            for t in range(PACK):
+                nc.tensor.matmul(bank[:, t, :], logs_b[u][:, t * P : (t + 1) * P], identity[:], start=(t == 0), stop=False, is_transpose=True)
+            for t in range(PACK):
+                nc.tensor.matmul(bank[:, t, :], logs_a[u][:, t * P : (t + 1) * P], identity[:], start=False, stop=(t == PACK - 1), is_transpose=True)
+            z_bf[u] = ring.tile([P, P, PACK], BF16, name="z_bf", bufs=3, align_bytes=64)
+            nc.vector.tensor_tensor(
+                z_bf[u][:].rearrange("p (c i) t -> p c t i", i=WALK),
+                bank[:].rearrange("p t (c i) -> p c t i", i=WALK),
+                weights[g, h][:, :, cols].rearrange("p t (c i) -> p c t i", i=WALK),
+                ALU.mult,
+            )
+
+        def quantize_z(u):
+            z_w[units[u]] = ring.tile([P, P], I32, name="z_w", bufs=16, align_bytes=64)
+            z_s[units[u]] = ring.tile([P, P], U8, name="z_s", bufs=16, align_bytes=64)
+            nc.vector.quantize_mx(
+                out=z_w[units[u]][:].bitcast(FP8X4), scales=z_s[units[u]][:], in_=z_bf[u][:].rearrange("p j t -> p (j t)")
+            )
+
+        def second_pass(b, g):
+            if g == 0:
+                y_bank[b] = psum.tile([P, PACK, P], F32, name="second", bufs=2)
+            for t in range(PACK):
+                nc.tensor.matmul_mx(
+                    out=y_bank[b][:, t, :],
+                    lhsT=w4_w[:, g, t, :].bitcast(FP4X4),
+                    lhsT_scale=w4_s[:, g, t, :],
+                    rhs=z_w[b, g][:].bitcast(FP8X4),
+                    rhs_scale=z_s[b, g][:],
+                    start=(g == 0 and t == 0),
+                    stop=(g == GROUPS - 1 and t == PACK - 1),
+                )
+
+        y_rows = out_0.rearrange("(p t) j -> p t j", t=PACK)
+        y_words = out_1[0].rearrange("p m t -> p (m t)").bitcast(I32)
+        chunks = [(0, 2), (2, 4), (4, 6), (6, 7), (7, 8)]
+
+        def finish(b):
+            first, last = [c for c in chunks if c[0] <= b < c[1]][0]
+            if b == first:
+                y_f32[first] = keep.tile([P, PACK, (last - first) * P], F32, name="y_f32_%d" % first)
+            part = y_f32[first][:, :, (b - first) * P : (b - first + 1) * P]
+            y_bf[b] = ring.tile([P, P, PACK], BF16, name="y_bf", bufs=2, align_bytes=64)
+            if b == BLOCKS - 1:
+                nc.vector.tensor_copy(out=y_bf[b][:], in_=y_bank[b][:].rearrange("p t j -> p j t"))
+                nc.scalar.copy(out=part, in_=y_bank[b][:])
+            else:
+                nc.vector.tensor_copy(out=part, in_=y_bank[b][:])
+                nc.vector.tensor_copy(
+                    out=y_bf[b][:].rearrange("p (c i) t -> p c t i", i=4), in_=part.rearrange("p t (c i) -> p c t i", i=4)
+                )
+            if b == last - 1:
+                nc.sync.dma_start(out=y_rows[:, :, first * P : last * P], in_=y_f32[first][:])
+
+        def quantize_y(b):
+            first, last = [c for c in chunks if c[0] <= b < c[1]][0]
+            cols = slice(b * P, (b + 1) * P)
+            nc.vector.quantize_mx(out=y_w[:, cols].bitcast(FP8X4), scales=y_s[:, cols], in_=y_bf[b][:].rearrange("p j t -> p (j t)"))
+            if b == last - 1:
+                nc.sync.dma_start(out=y_words[:, first * P : last * P], in_=y_w[:, first * P : last * P])
+
+        gather("b", 0)
+        gather("a", 0)
+        round_w1(0)
+        quantize_w1(0)
+        extra = {
+            1: [lambda: round_w1(1)],
+            2: [lambda: quantize_w1(1)],
+            4: [lambda: round_w1(2)],
+            5: [lambda: quantize_w1(2), deal_w4],
+            6: [lambda: gather("b", 1)],
+            9: [lambda: gather("a", 1)],
+        }
+
+        pending = None
+        square_step(0)
+        for s in range(len(steps)):
+            if s + 1 < len(steps):
+                square_step(s + 1)
+            log_step(s)
+            for side, u in steps[s]:
+                if side == "a":
+                    contrast(u)
+                    if u > 0:
+                        quantize_z(u - 1)
+                        b, g = units[u - 1]
+                        if b >= BLOCKS_PER_HALF:
+                            second_pass(b, g)
+                        elif g == GROUPS - 1:
+                            for g2 in range(GROUPS):
+                                second_pass(b, g2)
+                        if pending is not None:
+                            quantize_y(pending)
+                            pending = None
+                        if g == GROUPS - 1:
+                            finish(b)
+                            pending = b
+            for job in extra.get(s, []):
+                job()
+        quantize_z(len(units) - 1)
+        second_pass(BLOCKS - 1, GROUPS - 1)
+        finish(BLOCKS - 1)
+        quantize_y(BLOCKS - 1)
+        for q in range(4):
+            queue = nc.scalar if q % 2 else nc.sync
+            queue.dma_start(out=out_2[0, 4 * q : 4 * q + 4, :].bitcast(I32), in_=y_s[32 * q : 32 * q + 4, :].bitcast(I32))

@@ -24,8 +24,11 @@ HALF = 512
 HALVES = S // HALF
 BLOCKS = S // P
 BLOCKS_PER_HALF = HALF // P
-LEAD = 4
-WALK = 2
+LEAD = 6
+WALK = 4
+TURNED = (0,)
+SKIPS = (2, 5, 8, 11)
+VECTOR_SQUARES = ()
 
 
 def tile_list_codeshare_alliance_contrast_kernel(
@@ -43,14 +46,13 @@ def tile_list_codeshare_alliance_contrast_kernel(
         tab_w = keep.tile([P, T], U16, name="tab_w", align_bytes=64)
         tab_s = keep.tile([P, T], U8, name="tab_s", align_bytes=64)
         w8_first = keep.tile([P, PASS], I32, name="w8_first", align_bytes=64)
-        w8_s = keep.tile([P, H], U8, name="w8_s", align_bytes=64)
+        w8_raw_s = keep.tile([P, H], U8, name="w8_raw_s", align_bytes=64)
         w4_w = keep.tile([P, GROUPS, PACK, P], U16, name="w4_w", align_bytes=64)
         w4_s = keep.tile([P, GROUPS, PACK, P], U8, name="w4_s", align_bytes=64)
         w1_w = [keep.tile([P, PASS], I32, name="w1_w%d" % g, align_bytes=64) for g in range(GROUPS)]
         w1_s = [keep.tile([P, PASS], U8, name="w1_s%d" % g, align_bytes=64) for g in range(GROUPS)]
-        picked_w = {
-            (side, h): keep.tile([P, HALF], U16, name="picked_w%s%d" % (side, h), align_bytes=64) for side in "ab" for h in range(HALVES)
-        }
+        first_w = keep.tile([P, HALF], U16, name="first_w", align_bytes=64)
+        picked_w = {("b", 0): first_w[:]}
         picked_s = {
             (side, h): keep.tile([P, HALF], U8, name="picked_s%s%d" % (side, h), align_bytes=64) for side in "ab" for h in range(HALVES)
         }
@@ -62,15 +64,16 @@ def tile_list_codeshare_alliance_contrast_kernel(
 
         nc.vector.memset(warm_in[:], 1.0)
         nc.vector.memset(tab_s[:].bitcast(I32), 0)
-        nc.vector.memset(w8_s[:].bitcast(I32), 0)
+        nc.vector.memset(w8_raw_s[:].bitcast(I32), 0)
         nc.scalar.activation(out=warm_out[:], in_=warm_in[:], func=ACT.Ln, bias=1.0)
+        make_identity(nc, identity[:])
         piece = PACK * PASS
         floats = keep.tile([P, (GROUPS + GROUPS * HALVES) * piece], F32, name="floats", tag="floats", align_bytes=64)
         pieces = [floats[:, i * piece : (i + 1) * piece].rearrange("p (t c) -> p t c", t=PACK) for i in range(GROUPS + GROUPS * HALVES)]
         w1_raw = pieces[:GROUPS]
         weights = {(g, h): pieces[GROUPS + h * GROUPS + g] for g in range(GROUPS) for h in range(HALVES)}
         words = keep.tile([P, H - PASS + GROUPS * N // 2 + GROUPS * N // 4], I32, name="words", tag="words", align_bytes=64)
-        w8_w = [w8_first[:], words[:, 0:PASS], words[:, PASS : 2 * PASS]]
+        w8_raw_w = [w8_first[:], words[:, 0:PASS], words[:, PASS : 2 * PASS]]
         w4_raw_w = words[:, H - PASS : H - PASS + GROUPS * N // 2].rearrange("p (g c) -> p g c", g=GROUPS)
         w4_raw_s = words[:, H - PASS + GROUPS * N // 2 :]
         w8_rows = w8_words[0].rearrange("p c i -> p (c i)").bitcast(I32)
@@ -81,8 +84,7 @@ def tile_list_codeshare_alliance_contrast_kernel(
         for q in range(4):
             nc.sync.dma_start(out=tab_s[32 * q : 32 * q + 4, :].bitcast(I32), in_=tab_scales[0, 4 * q : 4 * q + 4, :].bitcast(I32))
         for q in range(4):
-            nc.sync.dma_start(out=w8_s[32 * q : 32 * q + 4, :].bitcast(I32), in_=w8_scales[0, 4 * q : 4 * q + 4, :].bitcast(I32))
-
+            nc.sync.dma_start(out=w8_raw_s[32 * q : 32 * q + 4, :].bitcast(I32), in_=w8_scales[0, 4 * q : 4 * q + 4, :].bitcast(I32))
 
         def load_w1(g):
             nc.sync.dma_start(out=w1_raw[g], in_=w1[:, g * PASS : (g + 1) * PASS].rearrange("(p t) c -> p t c", t=PACK))
@@ -91,11 +93,12 @@ def tile_list_codeshare_alliance_contrast_kernel(
             rows = traffic[g * PASS : (g + 1) * PASS, h * HALF : (h + 1) * HALF]
             nc.sync.dma_start(out=weights[g, h], in_=rows.rearrange("(p t) j -> p t j", t=PACK))
 
-        make_identity(nc, identity[:])
         load_w1(0)
         nc.sync.dma_start(out=words[:, 0 : H - PASS], in_=w8_rows[:, PASS:H])
         load_traffic(0, 0)
         load_w1(1)
+        load_traffic(1, 0)
+        load_w1(2)
         nc.sync.dma_start(out=w4_raw_w, in_=w4_words.rearrange("g p b -> p g b").bitcast(I32))
         nc.gpsimd.memset(w4_raw_s, 0)
         for q in range(4):
@@ -103,103 +106,168 @@ def tile_list_codeshare_alliance_contrast_kernel(
                 out=w4_raw_s[32 * q : 32 * q + 4, :].rearrange("q (g c) -> q g c", g=GROUPS),
                 in_=w4_scales[:, 4 * q : 4 * q + 4, :].rearrange("g q c -> q g c").bitcast(I32),
             )
-        load_traffic(1, 0)
-        load_w1(2)
         load_traffic(2, 0)
         for g in range(GROUPS):
             load_traffic(g, 1)
 
+        def entries(side, h):
+            return (list_a if side == "a" else list_b)[:, h * HALF // 16 : (h + 1) * HALF // 16]
 
-        def gather(side, h):
-            entries = (list_a if side == "a" else list_b)[:, h * HALF // 16 : (h + 1) * HALF // 16]
-            nc.vector.tensor_copy(picked_w[side, h][:], tab_w[:].indirect(entries))
-            nc.vector.tensor_copy(picked_s[side, h][:], tab_s[:].indirect(entries))
+        def gather_words(side, h):
+            nc.vector.tensor_copy(picked_w[side, h], tab_w[:].indirect(entries(side, h)))
+
+        def gather_scales(side, h):
+            nc.vector.tensor_copy(picked_s[side, h][:], tab_s[:].indirect(entries(side, h)))
 
         w1_bf = {}
 
         def round_w1(g):
-            w1_bf[g] = ring.tile([P, PASS, PACK], BF16, name="w1_bf", bufs=2, align_bytes=64)
-            nc.vector.tensor_copy(
-                out=w1_bf[g][:].rearrange("p (c i) t -> p c t i", i=4),
-                in_=w1_raw[g].rearrange("p t (c i) -> p c t i", i=4),
-            )
+            w1_bf[g] = keep.tile([P, PASS * PACK], BF16, name="w1_bf", tag="w1_bf" if g else "later_w", align_bytes=64)
+            if g in TURNED:
+                nc.vector.tensor_copy(
+                    out=w1_bf[g][:].rearrange("p (c i k) -> p c k i", i=4, k=PACK),
+                    in_=w1_raw[g].rearrange("p k (c i) -> p c k i", i=4),
+                )
+            else:
+                nc.vector.tensor_copy(
+                    out=w1_bf[g][:].rearrange("p (t m k) -> p m t k", t=PACK, k=PACK),
+                    in_=w1_raw[g].rearrange("p k (m t) -> p m t k", t=PACK),
+                )
 
         def quantize_w1(g):
-            nc.vector.quantize_mx(out=w1_w[g][:].bitcast(FP8X4), scales=w1_s[g][:], in_=w1_bf[g][:].rearrange("p c t -> p (c t)"))
+            nc.vector.quantize_mx(out=w1_w[g][:].bitcast(FP8X4), scales=w1_s[g][:], in_=w1_bf[g][:])
+
+        w8_w = {g: w8_raw_w[g] for g in TURNED}
+        w8_s = {g: w8_raw_s[:, g * PASS : (g + 1) * PASS] for g in TURNED}
+
+        def deal_w8(g):
+            dealt_w = keep.tile([P, PASS], I32, name="w8_dealt_w%d" % g, align_bytes=64)
+            dealt_s = keep.tile([P, PASS], U8, name="w8_dealt_s%d" % g, align_bytes=64)
+            nc.vector.tensor_copy(
+                out=dealt_w[:].rearrange("p (t c i) -> p c t i", t=PACK, i=4),
+                in_=w8_raw_w[g].rearrange("p (c i t) -> p c t i", i=4, t=PACK),
+            )
+            nc.vector.tensor_copy(
+                out=dealt_s[:].rearrange("p (t c i) -> p c t i", t=PACK, i=16),
+                in_=w8_raw_s[:, g * PASS : (g + 1) * PASS].rearrange("p (c i t) -> p c t i", i=16, t=PACK),
+            )
+            w8_w[g], w8_s[g] = dealt_w[:], dealt_s[:]
 
         def deal_w4():
-            for g in range(GROUPS):
-                nc.vector.tensor_copy(out=w4_w[:, g, :, :], in_=w4_raw_w[:, g, :].bitcast(U16).rearrange("p (m t) -> p t m", t=PACK))
-            nc.vector.tensor_copy(out=w4_s[:], in_=w4_raw_s.bitcast(U8).rearrange("p (g m t) -> p g t m", g=GROUPS, t=PACK))
+            nc.vector.tensor_copy(
+                out=w4_w[:].rearrange("p g t (c i) -> p g c t i", i=8),
+                in_=w4_raw_w.bitcast(U16).rearrange("p g (c i t) -> p g c t i", i=8, t=PACK),
+            )
+            nc.vector.tensor_copy(
+                out=w4_s[:].rearrange("p g t (c i) -> p g c t i", i=16),
+                in_=w4_raw_s.bitcast(U8).rearrange("p (g c i t) -> p g c t i", g=GROUPS, i=16, t=PACK),
+            )
 
         units = [(b, g) for g in range(GROUPS) for b in range(BLOCKS_PER_HALF)]
         units = units + [(b, g) for b in range(BLOCKS_PER_HALF, BLOCKS) for g in range(GROUPS)]
-        tasks = [("b", u) for u in range(LEAD)]
+        order_b = list(range(len(units)))
+        tasks = [("b", u) for u in order_b[:LEAD]]
         ahead = LEAD
         for u in range(len(units)):
             tasks.append(("a", u))
-            if ahead < len(units) and u not in (7, 14):
-                tasks.append(("b", ahead))
+            if ahead < len(units) and u not in SKIPS:
+                tasks.append(("b", order_b[ahead]))
                 ahead = ahead + 1
         steps = [tasks[i : i + 2] for i in range(0, len(tasks) - 2, 2)] + [tasks[-2:-1], tasks[-1:]]
 
-        squares, logs_a, logs_b, z_bf, z_w, z_s, y_bank, y_f32, y_bf = {}, {}, {}, {}, {}, {}, {}, {}, {}
+        squares, logs, differences, z_bf, z_w, z_s, y_bank, y_f32, y_bf = {}, {}, {}, {}, {}, {}, {}, {}, {}
+
+        def place(u):
+            b, g = units[u]
+            return g, b // BLOCKS_PER_HALF, slice((b % BLOCKS_PER_HALF) * P, (b % BLOCKS_PER_HALF + 1) * P)
 
         def first_product(side, u, target):
-            b, g = units[u]
-            h, cols = b // BLOCKS_PER_HALF, slice((b % BLOCKS_PER_HALF) * P, (b % BLOCKS_PER_HALF + 1) * P)
+            g, h, cols = place(u)
             bank = psum.tile([P, PASS], F32, name="first", bufs=4)
-            nc.tensor.matmul_mx(
-                out=bank[:],
-                lhsT=picked_w[side, h][:, cols].bitcast(FP4X4),
-                lhsT_scale=picked_s[side, h][:, cols],
-                rhs=(w1_w[g][:] if side == "a" else w8_w[g]).bitcast(FP8X4),
-                rhs_scale=w1_s[g][:] if side == "a" else w8_s[:, g * PASS : (g + 1) * PASS],
-                start=True,
-                stop=True,
-            )
-            nc.scalar.activation(
-                out=target.rearrange("p (t m) -> p t m", t=PACK), in_=bank[:].rearrange("p (m t) -> p t m", t=PACK), func=ACT.Square
-            )
+            weight_w, weight_s = (w1_w[g][:], w1_s[g][:]) if side == "a" else (w8_w[g], w8_s[g])
+            table_w, table_s = picked_w[side, h][:, cols].bitcast(FP4X4), picked_s[side, h][:, cols]
+            if g in TURNED:
+                nc.tensor.matmul_mx(
+                    out=bank[:], lhsT=table_w, lhsT_scale=table_s, rhs=weight_w.bitcast(FP8X4), rhs_scale=weight_s, start=True, stop=True
+                )
+                source = bank[:].rearrange("p (m t) -> p t m", t=PACK)
+            else:
+                for t in range(PACK):
+                    rows = slice(t * P, (t + 1) * P)
+                    nc.tensor.matmul_mx(
+                        out=bank[:, rows],
+                        lhsT=weight_w[:, rows].bitcast(FP8X4),
+                        lhsT_scale=weight_s[:, rows],
+                        rhs=table_w,
+                        rhs_scale=table_s,
+                        start=True,
+                        stop=True,
+                    )
+                source = bank[:].rearrange("p (t m) -> p t m", t=PACK)
+            if side == "b" and u in VECTOR_SQUARES:
+                plain = ring.tile([P, PACK, P], F32, name="plain", bufs=1)
+                nc.vector.tensor_copy(out=plain[:], in_=source)
+                nc.vector.tensor_tensor(target, source, plain[:], ALU.mult)
+            else:
+                nc.scalar.activation(out=target, in_=source, func=ACT.Square)
 
-        def square_step(s):
-            squares[s] = ring.tile([P, 2, PASS], F32, name="squares", bufs=3)
+        def square_step(s, early):
+            if s not in squares:
+                squares[s] = ring.tile([P, 2, PACK, P], F32, name="squares", bufs=4)
             for k, (side, u) in enumerate(steps[s]):
-                first_product(side, u, squares[s][:, k, :])
+                if (side == "b" and u in VECTOR_SQUARES) == early:
+                    first_product(side, u, squares[s][:, k, :, :])
 
         def log_step(s):
-            logs = ring.tile([P, 2, PASS], F32, name="logs", bufs=4)
-            nc.scalar.activation(out=logs[:, 0 : len(steps[s]), :], in_=squares[s][:, 0 : len(steps[s]), :], func=ACT.Ln, bias=1.0)
+            both = ring.tile([P, 2, PACK, P], F32, name="logs", bufs=9)
+            count = len(steps[s])
+            nc.scalar.activation(out=both[:, 0:count, :, :], in_=squares[s][:, 0:count, :, :], func=ACT.Ln, bias=1.0)
             for k, (side, u) in enumerate(steps[s]):
-                if side == "a":
-                    logs_a[u] = logs[:, k, :]
-                else:
-                    negated = ring.tile([P, PASS], F32, name="negated", bufs=LEAD + 3)
-                    nc.gpsimd.tensor_scalar(negated[:], logs[:, k, :], -1.0, 0.0, ALU.mult, ALU.add)
-                    logs_b[u] = negated[:]
+                logs[side, u] = both[:, k, :, :]
+                if side == "b" and units[u][1] in TURNED:
+                    nc.vector.tensor_scalar(logs[side, u], logs[side, u], -1.0, 0.0, ALU.mult, ALU.add)
 
-        def contrast(u):
-            b, g = units[u]
-            h, cols = b // BLOCKS_PER_HALF, slice((b % BLOCKS_PER_HALF) * P, (b % BLOCKS_PER_HALF + 1) * P)
-            bank = psum.tile([P, PACK, P], F32, name="difference", bufs=2)
-            for t in range(PACK):
-                nc.tensor.matmul(bank[:, t, :], logs_b[u][:, t * P : (t + 1) * P], identity[:], start=(t == 0), stop=False, is_transpose=True)
-            for t in range(PACK):
-                nc.tensor.matmul(bank[:, t, :], logs_a[u][:, t * P : (t + 1) * P], identity[:], start=False, stop=(t == PACK - 1), is_transpose=True)
-            z_bf[u] = ring.tile([P, P, PACK], BF16, name="z_bf", bufs=3, align_bytes=64)
+        def subtract(u):
+            if units[u][1] in TURNED:
+                differences[u] = psum.tile([P, PACK, P], F32, name="turned", bufs=2)
+                for side in "ba":
+                    for t in range(PACK):
+                        nc.tensor.matmul(
+                            differences[u][:, t, :],
+                            logs[side, u][:, t, :],
+                            identity[:],
+                            start=(side == "b" and t == 0),
+                            stop=(side == "a" and t == PACK - 1),
+                            is_transpose=True,
+                        )
+            else:
+                differences[u] = ring.tile([P, PACK, P], F32, name="difference", bufs=2)
+                nc.vector.tensor_tensor(differences[u][:], logs["a", u], logs["b", u], ALU.subtract)
+
+        def weigh(u):
+            g, h, cols = place(u)
+            if u % 2 == 0:
+                z_bf[u] = ring.tile([P, 2, P, PACK], BF16, name="z_bf", bufs=3, align_bytes=64)
             nc.vector.tensor_tensor(
-                z_bf[u][:].rearrange("p (c i) t -> p c t i", i=WALK),
-                bank[:].rearrange("p t (c i) -> p c t i", i=WALK),
+                z_bf[u - u % 2][:, u % 2, :, :].rearrange("p (c i) t -> p c t i", i=WALK),
+                differences[u][:].rearrange("p t (c i) -> p c t i", i=WALK),
                 weights[g, h][:, :, cols].rearrange("p t (c i) -> p c t i", i=WALK),
                 ALU.mult,
             )
 
-        def quantize_z(u):
-            z_w[units[u]] = ring.tile([P, P], I32, name="z_w", bufs=16, align_bytes=64)
-            z_s[units[u]] = ring.tile([P, P], U8, name="z_s", bufs=16, align_bytes=64)
-            nc.vector.quantize_mx(
-                out=z_w[units[u]][:].bitcast(FP8X4), scales=z_s[units[u]][:], in_=z_bf[u][:].rearrange("p j t -> p (j t)")
-            )
+        def quantize_z(u, first, count):
+            codes = ring.tile([P, count * P], I32, name="z_w", bufs=8, align_bytes=64)
+            plane = ring.tile([P, count * P], U8, name="z_s", bufs=8, align_bytes=64)
+            source = z_bf[u][:, first : first + count, :, :].rearrange("p k j t -> p (k j t)")
+            nc.vector.quantize_mx(out=codes[:].bitcast(FP8X4), scales=plane[:], in_=source)
+            for k in range(count):
+                z_w[units[u + first + k]], z_s[units[u + first + k]] = codes[:, k * P : (k + 1) * P], plane[:, k * P : (k + 1) * P]
+                b, g = units[u + first + k]
+                if b >= BLOCKS_PER_HALF:
+                    second_pass(b, g)
+                elif g == GROUPS - 1:
+                    for earlier in range(GROUPS):
+                        second_pass(b, earlier)
 
         def second_pass(b, g):
             if g == 0:
@@ -209,8 +277,8 @@ def tile_list_codeshare_alliance_contrast_kernel(
                     out=y_bank[b][:, t, :],
                     lhsT=w4_w[:, g, t, :].bitcast(FP4X4),
                     lhsT_scale=w4_s[:, g, t, :],
-                    rhs=z_w[b, g][:].bitcast(FP8X4),
-                    rhs_scale=z_s[b, g][:],
+                    rhs=z_w[b, g].bitcast(FP8X4),
+                    rhs_scale=z_s[b, g],
                     start=(g == 0 and t == 0),
                     stop=(g == GROUPS - 1 and t == PACK - 1),
                 )
@@ -222,17 +290,16 @@ def tile_list_codeshare_alliance_contrast_kernel(
         def finish(b):
             first, last = [c for c in chunks if c[0] <= b < c[1]][0]
             if b == first:
-                y_f32[first] = keep.tile([P, PACK, (last - first) * P], F32, name="y_f32_%d" % first)
+                y_f32[first] = ring.tile([P, PACK, (last - first) * P], F32, name="y_f32", bufs=2)
             part = y_f32[first][:, :, (b - first) * P : (b - first + 1) * P]
             y_bf[b] = ring.tile([P, P, PACK], BF16, name="y_bf", bufs=2, align_bytes=64)
             if b == BLOCKS - 1:
-                nc.vector.tensor_copy(out=y_bf[b][:], in_=y_bank[b][:].rearrange("p t j -> p j t"))
                 nc.scalar.copy(out=part, in_=y_bank[b][:])
             else:
                 nc.vector.tensor_copy(out=part, in_=y_bank[b][:])
-                nc.vector.tensor_copy(
-                    out=y_bf[b][:].rearrange("p (c i) t -> p c t i", i=4), in_=part.rearrange("p t (c i) -> p c t i", i=4)
-                )
+            nc.vector.tensor_copy(
+                out=y_bf[b][:].rearrange("p (c i) t -> p c t i", i=4), in_=part.rearrange("p t (c i) -> p c t i", i=4)
+            )
             if b == last - 1:
                 nc.sync.dma_start(out=y_rows[:, :, first * P : last * P], in_=y_f32[first][:])
 
@@ -243,48 +310,58 @@ def tile_list_codeshare_alliance_contrast_kernel(
             if b == last - 1:
                 nc.sync.dma_start(out=y_words[:, first * P : last * P], in_=y_w[:, first * P : last * P])
 
-        gather("b", 0)
-        gather("a", 0)
+        def vector_round(u):
+            if u < len(units):
+                subtract(u)
+            done = u - 2
+            if done >= len(units) - 2 and done < len(units):
+                quantize_z(len(units) - 2, done % 2, 1)
+            elif 0 <= done < len(units) and done % 2 == 1:
+                quantize_z(done - 1, 0, 2)
+            if 0 <= u - 1 < len(units):
+                weigh(u - 1)
+            if 0 <= u - 5 < len(units) and units[u - 5][1] == GROUPS - 1:
+                quantize_y(units[u - 5][0])
+            if 0 <= u - 4 < len(units) and units[u - 4][1] == GROUPS - 1:
+                finish(units[u - 4][0])
+
+        gather_words("b", 0)
+        gather_scales("b", 0)
+        gather_scales("a", 0)
+        deal_w8(1)
         round_w1(0)
         quantize_w1(0)
-        extra = {
-            1: [lambda: round_w1(1)],
-            2: [lambda: quantize_w1(1)],
-            4: [lambda: round_w1(2)],
-            5: [lambda: quantize_w1(2), deal_w4],
-            6: [lambda: gather("b", 1)],
-            9: [lambda: gather("a", 1)],
-        }
+        later_w = keep.tile([P, 3, HALF], U16, name="later_w", tag="later_w", align_bytes=64)
+        for i, key in enumerate([("a", 0), ("b", 1), ("a", 1)]):
+            picked_w[key] = later_w[:, i, :]
+        gather_words("a", 0)
+        deal_w8(2)
 
-        pending = None
-        square_step(0)
+        def prepare(s):
+            if s in (1, 4):
+                round_w1(1 + s // 4)
+            if s in (2, 5):
+                quantize_w1(1 + s // 4)
+            if s in (6, 8):
+                side = "b" if s == 6 else "a"
+                gather_words(side, 1)
+                gather_scales(side, 1)
+            if s == 7:
+                deal_w4()
+
+        square_step(0, False)
         for s in range(len(steps)):
+            if s + 2 < len(steps):
+                square_step(s + 2, True)
             if s + 1 < len(steps):
-                square_step(s + 1)
+                square_step(s + 1, False)
             log_step(s)
             for side, u in steps[s]:
                 if side == "a":
-                    contrast(u)
-                    if u > 0:
-                        quantize_z(u - 1)
-                        b, g = units[u - 1]
-                        if b >= BLOCKS_PER_HALF:
-                            second_pass(b, g)
-                        elif g == GROUPS - 1:
-                            for g2 in range(GROUPS):
-                                second_pass(b, g2)
-                        if pending is not None:
-                            quantize_y(pending)
-                            pending = None
-                        if g == GROUPS - 1:
-                            finish(b)
-                            pending = b
-            for job in extra.get(s, []):
-                job()
-        quantize_z(len(units) - 1)
-        second_pass(BLOCKS - 1, GROUPS - 1)
-        finish(BLOCKS - 1)
-        quantize_y(BLOCKS - 1)
+                    vector_round(u)
+            prepare(s)
+        for u in range(len(units), len(units) + 5):
+            vector_round(u)
         for q in range(4):
             queue = nc.scalar if q % 2 else nc.sync
             queue.dma_start(out=out_2[0, 4 * q : 4 * q + 4, :].bitcast(I32), in_=y_s[32 * q : 32 * q + 4, :].bitcast(I32))

@@ -27,8 +27,8 @@ BLOCKS_PER_HALF = HALF // P
 LEAD = 6
 WALK = 4
 TURNED = (0,)
-SKIPS = (2, 5, 8, 11)
-VECTOR_SQUARES = ()
+SKIPS = (2, 4, 6, 8, 10)
+VECTOR_SQUARES = (14, 16, 18)
 
 
 def tile_list_codeshare_alliance_contrast_kernel(
@@ -173,7 +173,8 @@ def tile_list_codeshare_alliance_contrast_kernel(
             if ahead < len(units) and u not in SKIPS:
                 tasks.append(("b", order_b[ahead]))
                 ahead = ahead + 1
-        steps = [tasks[i : i + 2] for i in range(0, len(tasks) - 2, 2)] + [tasks[-2:-1], tasks[-1:]]
+        cuts = [0, 2, 4, 6] + list(range(8, len(tasks) - 4, 4)) + [len(tasks) - 4, len(tasks) - 2, len(tasks)]
+        steps = [tasks[first:last] for first, last in zip(cuts, cuts[1:])]
 
         squares, logs, differences, z_bf, z_w, z_s, y_bank, y_f32, y_bf = {}, {}, {}, {}, {}, {}, {}, {}, {}
 
@@ -183,7 +184,7 @@ def tile_list_codeshare_alliance_contrast_kernel(
 
         def first_product(side, u, target):
             g, h, cols = place(u)
-            bank = psum.tile([P, PASS], F32, name="first", bufs=4)
+            bank = psum.tile([P, PASS], F32, name="first", bufs=5)
             weight_w, weight_s = (w1_w[g][:], w1_s[g][:]) if side == "a" else (w8_w[g], w8_s[g])
             table_w, table_s = picked_w[side, h][:, cols].bitcast(FP4X4), picked_s[side, h][:, cols]
             if g in TURNED:
@@ -211,17 +212,14 @@ def tile_list_codeshare_alliance_contrast_kernel(
             else:
                 nc.scalar.activation(out=target, in_=source, func=ACT.Square)
 
-        def square_step(s, early):
-            if s not in squares:
-                squares[s] = ring.tile([P, 2, PACK, P], F32, name="squares", bufs=4)
+        def square_step(s):
+            squares[s] = ring.tile([P, len(steps[s]), PACK, P], F32, name="squares", bufs=3)
             for k, (side, u) in enumerate(steps[s]):
-                if (side == "b" and u in VECTOR_SQUARES) == early:
-                    first_product(side, u, squares[s][:, k, :, :])
+                first_product(side, u, squares[s][:, k, :, :])
 
         def log_step(s):
-            both = ring.tile([P, 2, PACK, P], F32, name="logs", bufs=9)
-            count = len(steps[s])
-            nc.scalar.activation(out=both[:, 0:count, :, :], in_=squares[s][:, 0:count, :, :], func=ACT.Ln, bias=1.0)
+            both = ring.tile([P, len(steps[s]), PACK, P], F32, name="logs%d" % len(steps[s]), bufs=4)
+            nc.scalar.activation(out=both[:], in_=squares[s][:], func=ACT.Ln, bias=1.0)
             for k, (side, u) in enumerate(steps[s]):
                 logs[side, u] = both[:, k, :, :]
                 if side == "b" and units[u][1] in TURNED:
@@ -229,7 +227,7 @@ def tile_list_codeshare_alliance_contrast_kernel(
 
         def subtract(u):
             if units[u][1] in TURNED:
-                differences[u] = psum.tile([P, PACK, P], F32, name="turned", bufs=2)
+                differences[u] = psum.tile([P, PACK, P], F32, name="turned", bufs=1)
                 for side in "ba":
                     for t in range(PACK):
                         nc.tensor.matmul(
@@ -338,23 +336,21 @@ def tile_list_codeshare_alliance_contrast_kernel(
         deal_w8(2)
 
         def prepare(s):
-            if s in (1, 4):
-                round_w1(1 + s // 4)
-            if s in (2, 5):
-                quantize_w1(1 + s // 4)
-            if s in (6, 8):
-                side = "b" if s == 6 else "a"
+            if s in (1, 3):
+                round_w1(1 + s // 3)
+            if s in (2, 3):
+                quantize_w1(s - 1)
+            if s in (4, 5):
+                side = "b" if s == 4 else "a"
                 gather_words(side, 1)
                 gather_scales(side, 1)
-            if s == 7:
+            if s == 6:
                 deal_w4()
 
-        square_step(0, False)
+        square_step(0)
         for s in range(len(steps)):
-            if s + 2 < len(steps):
-                square_step(s + 2, True)
             if s + 1 < len(steps):
-                square_step(s + 1, False)
+                square_step(s + 1)
             log_step(s)
             for side, u in steps[s]:
                 if side == "a":

from contextlib import ExitStack

import concourse.mybir as mybir
from concourse.masks import make_identity

K, T, S, H, N = 512, 4096, 1024, 1536, 512
FLOPS = 2 * K * H * S * 2 + 2 * H * N * S

F32 = mybir.dt.float32
BF16 = mybir.dt.bfloat16
I32 = mybir.dt.int32
U16 = mybir.dt.uint16
U8 = mybir.dt.uint8
FP8X4 = mybir.dt.float8_e4m3fn_x4
FP4X4 = mybir.dt.float4_e2m1fn_x4
ACT = mybir.ActivationFunctionType
ALU = mybir.AluOpType

P = 128
PACK = 4
PASS = P * PACK
GROUPS = H // PASS
HALF = 512
HALVES = S // HALF
BLOCKS = S // P
BLOCKS_PER_HALF = HALF // P
LEAD = 6
WALK = 4
TURNED = (0,)
SKIPS = (2, 4, 6, 8, 10)
VECTOR_SQUARES = (14, 16, 18)


def tile_list_codeshare_alliance_contrast_kernel(
    tc, tab_words, tab_scales, offs, offs2, w1, w8_words, w8_scales, traffic, w4_words, w4_scales, out_0, out_1, out_2
):
    nc = tc.nc
    with ExitStack() as ctx:
        lists = ctx.enter_context(tc.tile_pool(name="lists", bufs=1))
        keep = ctx.enter_context(tc.tile_pool(name="keep", bufs=1))
        ring = ctx.enter_context(tc.tile_pool(name="ring", bufs=1))
        psum = ctx.enter_context(tc.psum_pool(name="psum", bufs=1))

        list_a = lists.tile([P, S // 16], U16, name="list_a")
        list_b = lists.tile([P, S // 16], U16, name="list_b")
        tab_w = keep.tile([P, T], U16, name="tab_w", align_bytes=64)
        tab_s = keep.tile([P, T], U8, name="tab_s", align_bytes=64)
        w8_first = keep.tile([P, PASS], I32, name="w8_first", align_bytes=64)
        w8_raw_s = keep.tile([P, H], U8, name="w8_raw_s", align_bytes=64)
        w4_w = keep.tile([P, GROUPS, PACK, P], U16, name="w4_w", align_bytes=64)
        w4_s = keep.tile([P, GROUPS, PACK, P], U8, name="w4_s", align_bytes=64)
        w1_w = [keep.tile([P, PASS], I32, name="w1_w%d" % g, align_bytes=64) for g in range(GROUPS)]
        w1_s = [keep.tile([P, PASS], U8, name="w1_s%d" % g, align_bytes=64) for g in range(GROUPS)]
        first_w = keep.tile([P, HALF], U16, name="first_w", align_bytes=64)
        picked_w = {("b", 0): first_w[:]}
        picked_s = {
            (side, h): keep.tile([P, HALF], U8, name="picked_s%s%d" % (side, h), align_bytes=64) for side in "ab" for h in range(HALVES)
        }
        identity = keep.tile([P, P], F32, name="identity")
        y_w = keep.tile([P, S], I32, name="y_w", align_bytes=64)
        y_s = keep.tile([P, S], U8, name="y_s", align_bytes=64)
        warm_in = keep.tile([P, 1], F32, name="warm_in", tag="floats", align_bytes=64)
        warm_out = keep.tile([P, 1], F32, name="warm_out", tag="words", align_bytes=64)

        nc.vector.memset(warm_in[:], 1.0)
        nc.vector.memset(tab_s[:].bitcast(I32), 0)
        nc.vector.memset(w8_raw_s[:].bitcast(I32), 0)
        nc.scalar.activation(out=warm_out[:], in_=warm_in[:], func=ACT.Ln, bias=1.0)
        make_identity(nc, identity[:])
        piece = PACK * PASS
        floats = keep.tile([P, (GROUPS + GROUPS * HALVES) * piece], F32, name="floats", tag="floats", align_bytes=64)
        pieces = [floats[:, i * piece : (i + 1) * piece].rearrange("p (t c) -> p t c", t=PACK) for i in range(GROUPS + GROUPS * HALVES)]
        w1_raw = pieces[:GROUPS]
        weights = {(g, h): pieces[GROUPS + h * GROUPS + g] for g in range(GROUPS) for h in range(HALVES)}
        words = keep.tile([P, H - PASS + GROUPS * N // 2 + GROUPS * N // 4], I32, name="words", tag="words", align_bytes=64)
        w8_raw_w = [w8_first[:], words[:, 0:PASS], words[:, PASS : 2 * PASS]]
        w4_raw_w = words[:, H - PASS : H - PASS + GROUPS * N // 2].rearrange("p (g c) -> p g c", g=GROUPS)
        w4_raw_s = words[:, H - PASS + GROUPS * N // 2 :]
        w8_rows = w8_words[0].rearrange("p c i -> p (c i)").bitcast(I32)
        nc.sync.dma_start(list_b[:], offs2)
        nc.sync.dma_start(list_a[:], offs)
        nc.sync.dma_start(out=tab_w[:].bitcast(I32), in_=tab_words[0].bitcast(I32))
        nc.sync.dma_start(out=w8_first[:], in_=w8_rows[:, 0:PASS])
        for q in range(4):
            nc.sync.dma_start(out=tab_s[32 * q : 32 * q + 4, :].bitcast(I32), in_=tab_scales[0, 4 * q : 4 * q + 4, :].bitcast(I32))
        for q in range(4):
            nc.sync.dma_start(out=w8_raw_s[32 * q : 32 * q + 4, :].bitcast(I32), in_=w8_scales[0, 4 * q : 4 * q + 4, :].bitcast(I32))

        def load_w1(g):
            nc.sync.dma_start(out=w1_raw[g], in_=w1[:, g * PASS : (g + 1) * PASS].rearrange("(p t) c -> p t c", t=PACK))

        def load_traffic(g, h):
            rows = traffic[g * PASS : (g + 1) * PASS, h * HALF : (h + 1) * HALF]
            nc.sync.dma_start(out=weights[g, h], in_=rows.rearrange("(p t) j -> p t j", t=PACK))

        load_w1(0)
        nc.sync.dma_start(out=words[:, 0 : H - PASS], in_=w8_rows[:, PASS:H])
        load_traffic(0, 0)
        load_w1(1)
        load_traffic(1, 0)
        load_w1(2)
        nc.sync.dma_start(out=w4_raw_w, in_=w4_words.rearrange("g p b -> p g b").bitcast(I32))
        nc.gpsimd.memset(w4_raw_s, 0)
        for q in range(4):
            nc.sync.dma_start(
                out=w4_raw_s[32 * q : 32 * q + 4, :].rearrange("q (g c) -> q g c", g=GROUPS),
                in_=w4_scales[:, 4 * q : 4 * q + 4, :].rearrange("g q c -> q g c").bitcast(I32),
            )
        load_traffic(2, 0)
        for g in range(GROUPS):
            load_traffic(g, 1)

        def entries(side, h):
            return (list_a if side == "a" else list_b)[:, h * HALF // 16 : (h + 1) * HALF // 16]

        def gather_words(side, h):
            nc.vector.tensor_copy(picked_w[side, h], tab_w[:].indirect(entries(side, h)))

        def gather_scales(side, h):
            nc.vector.tensor_copy(picked_s[side, h][:], tab_s[:].indirect(entries(side, h)))

        w1_bf = {}

        def round_w1(g):
            w1_bf[g] = keep.tile([P, PASS * PACK], BF16, name="w1_bf", tag="w1_bf" if g else "later_w", align_bytes=64)
            if g in TURNED:
                nc.vector.tensor_copy(
                    out=w1_bf[g][:].rearrange("p (c i k) -> p c k i", i=4, k=PACK),
                    in_=w1_raw[g].rearrange("p k (c i) -> p c k i", i=4),
                )
            else:
                nc.vector.tensor_copy(
                    out=w1_bf[g][:].rearrange("p (t m k) -> p m t k", t=PACK, k=PACK),
                    in_=w1_raw[g].rearrange("p k (m t) -> p m t k", t=PACK),
                )

        def quantize_w1(g):
            nc.vector.quantize_mx(out=w1_w[g][:].bitcast(FP8X4), scales=w1_s[g][:], in_=w1_bf[g][:])

        w8_w = {g: w8_raw_w[g] for g in TURNED}
        w8_s = {g: w8_raw_s[:, g * PASS : (g + 1) * PASS] for g in TURNED}

        def deal_w8(g):
            dealt_w = keep.tile([P, PASS], I32, name="w8_dealt_w%d" % g, align_bytes=64)
            dealt_s = keep.tile([P, PASS], U8, name="w8_dealt_s%d" % g, align_bytes=64)
            nc.vector.tensor_copy(
                out=dealt_w[:].rearrange("p (t c i) -> p c t i", t=PACK, i=4),
                in_=w8_raw_w[g].rearrange("p (c i t) -> p c t i", i=4, t=PACK),
            )
            nc.vector.tensor_copy(
                out=dealt_s[:].rearrange("p (t c i) -> p c t i", t=PACK, i=16),
                in_=w8_raw_s[:, g * PASS : (g + 1) * PASS].rearrange("p (c i t) -> p c t i", i=16, t=PACK),
            )
            w8_w[g], w8_s[g] = dealt_w[:], dealt_s[:]

        def deal_w4():
            nc.vector.tensor_copy(
                out=w4_w[:].rearrange("p g t (c i) -> p g c t i", i=8),
                in_=w4_raw_w.bitcast(U16).rearrange("p g (c i t) -> p g c t i", i=8, t=PACK),
            )
            nc.vector.tensor_copy(
                out=w4_s[:].rearrange("p g t (c i) -> p g c t i", i=16),
                in_=w4_raw_s.bitcast(U8).rearrange("p (g c i t) -> p g c t i", g=GROUPS, i=16, t=PACK),
            )

        units = [(b, g) for g in range(GROUPS) for b in range(BLOCKS_PER_HALF)]
        units = units + [(b, g) for b in range(BLOCKS_PER_HALF, BLOCKS) for g in range(GROUPS)]
        order_b = list(range(len(units)))
        tasks = [("b", u) for u in order_b[:LEAD]]
        ahead = LEAD
        for u in range(len(units)):
            tasks.append(("a", u))
            if ahead < len(units) and u not in SKIPS:
                tasks.append(("b", order_b[ahead]))
                ahead = ahead + 1
        cuts = [0, 2, 4, 6] + list(range(8, len(tasks) - 4, 4)) + [len(tasks) - 4, len(tasks) - 2, len(tasks)]
        steps = [tasks[first:last] for first, last in zip(cuts, cuts[1:])]

        squares, logs, differences, z_bf, z_w, z_s, y_bank, y_f32, y_bf = {}, {}, {}, {}, {}, {}, {}, {}, {}

        def place(u):
            b, g = units[u]
            return g, b // BLOCKS_PER_HALF, slice((b % BLOCKS_PER_HALF) * P, (b % BLOCKS_PER_HALF + 1) * P)

        def first_product(side, u, target):
            g, h, cols = place(u)
            bank = psum.tile([P, PASS], F32, name="first", bufs=5)
            weight_w, weight_s = (w1_w[g][:], w1_s[g][:]) if side == "a" else (w8_w[g], w8_s[g])
            table_w, table_s = picked_w[side, h][:, cols].bitcast(FP4X4), picked_s[side, h][:, cols]
            if g in TURNED:
                nc.tensor.matmul_mx(
                    out=bank[:], lhsT=table_w, lhsT_scale=table_s, rhs=weight_w.bitcast(FP8X4), rhs_scale=weight_s, start=True, stop=True
                )
                source = bank[:].rearrange("p (m t) -> p t m", t=PACK)
            else:
                for t in range(PACK):
                    rows = slice(t * P, (t + 1) * P)
                    nc.tensor.matmul_mx(
                        out=bank[:, rows],
                        lhsT=weight_w[:, rows].bitcast(FP8X4),
                        lhsT_scale=weight_s[:, rows],
                        rhs=table_w,
                        rhs_scale=table_s,
                        start=True,
                        stop=True,
                    )
                source = bank[:].rearrange("p (t m) -> p t m", t=PACK)
            if side == "b" and u in VECTOR_SQUARES:
                plain = ring.tile([P, PACK, P], F32, name="plain", bufs=1)
                nc.vector.tensor_copy(out=plain[:], in_=source)
                nc.vector.tensor_tensor(target, source, plain[:], ALU.mult)
            else:
                nc.scalar.activation(out=target, in_=source, func=ACT.Square)

        def square_step(s):
            squares[s] = ring.tile([P, len(steps[s]), PACK, P], F32, name="squares", bufs=3)
            for k, (side, u) in enumerate(steps[s]):
                first_product(side, u, squares[s][:, k, :, :])

        def log_step(s):
            both = ring.tile([P, len(steps[s]), PACK, P], F32, name="logs%d" % len(steps[s]), bufs=4)
            nc.scalar.activation(out=both[:], in_=squares[s][:], func=ACT.Ln, bias=1.0)
            for k, (side, u) in enumerate(steps[s]):
                logs[side, u] = both[:, k, :, :]
                if side == "b" and units[u][1] in TURNED:
                    nc.vector.tensor_scalar(logs[side, u], logs[side, u], -1.0, 0.0, ALU.mult, ALU.add)

        def subtract(u):
            if units[u][1] in TURNED:
                differences[u] = psum.tile([P, PACK, P], F32, name="turned", bufs=1)
                for side in "ba":
                    for t in range(PACK):
                        nc.tensor.matmul(
                            differences[u][:, t, :],
                            logs[side, u][:, t, :],
                            identity[:],
                            start=(side == "b" and t == 0),
                            stop=(side == "a" and t == PACK - 1),
                            is_transpose=True,
                        )
            else:
                differences[u] = ring.tile([P, PACK, P], F32, name="difference", bufs=2)
                nc.vector.tensor_tensor(differences[u][:], logs["a", u], logs["b", u], ALU.subtract)

        def weigh(u):
            g, h, cols = place(u)
            if u % 2 == 0:
                z_bf[u] = ring.tile([P, 2, P, PACK], BF16, name="z_bf", bufs=3, align_bytes=64)
            nc.vector.tensor_tensor(
                z_bf[u - u % 2][:, u % 2, :, :].rearrange("p (c i) t -> p c t i", i=WALK),
                differences[u][:].rearrange("p t (c i) -> p c t i", i=WALK),
                weights[g, h][:, :, cols].rearrange("p t (c i) -> p c t i", i=WALK),
                ALU.mult,
            )

        def quantize_z(u, first, count):
            codes = ring.tile([P, count * P], I32, name="z_w", bufs=8, align_bytes=64)
            plane = ring.tile([P, count * P], U8, name="z_s", bufs=8, align_bytes=64)
            source = z_bf[u][:, first : first + count, :, :].rearrange("p k j t -> p (k j t)")
            nc.vector.quantize_mx(out=codes[:].bitcast(FP8X4), scales=plane[:], in_=source)
            for k in range(count):
                z_w[units[u + first + k]], z_s[units[u + first + k]] = codes[:, k * P : (k + 1) * P], plane[:, k * P : (k + 1) * P]
                b, g = units[u + first + k]
                if b >= BLOCKS_PER_HALF:
                    second_pass(b, g)
                elif g == GROUPS - 1:
                    for earlier in range(GROUPS):
                        second_pass(b, earlier)

        def second_pass(b, g):
            if g == 0:
                y_bank[b] = psum.tile([P, PACK, P], F32, name="second", bufs=2)
            for t in range(PACK):
                nc.tensor.matmul_mx(
                    out=y_bank[b][:, t, :],
                    lhsT=w4_w[:, g, t, :].bitcast(FP4X4),
                    lhsT_scale=w4_s[:, g, t, :],
                    rhs=z_w[b, g].bitcast(FP8X4),
                    rhs_scale=z_s[b, g],
                    start=(g == 0 and t == 0),
                    stop=(g == GROUPS - 1 and t == PACK - 1),
                )

        y_rows = out_0.rearrange("(p t) j -> p t j", t=PACK)
        y_words = out_1[0].rearrange("p m t -> p (m t)").bitcast(I32)
        chunks = [(0, 2), (2, 4), (4, 6), (6, 7), (7, 8)]

        def finish(b):
            first, last = [c for c in chunks if c[0] <= b < c[1]][0]
            if b == first:
                y_f32[first] = ring.tile([P, PACK, (last - first) * P], F32, name="y_f32", bufs=2)
            part = y_f32[first][:, :, (b - first) * P : (b - first + 1) * P]
            y_bf[b] = ring.tile([P, P, PACK], BF16, name="y_bf", bufs=2, align_bytes=64)
            if b == BLOCKS - 1:
                nc.scalar.copy(out=part, in_=y_bank[b][:])
            else:
                nc.vector.tensor_copy(out=part, in_=y_bank[b][:])
            nc.vector.tensor_copy(
                out=y_bf[b][:].rearrange("p (c i) t -> p c t i", i=4), in_=part.rearrange("p t (c i) -> p c t i", i=4)
            )
            if b == last - 1:
                nc.sync.dma_start(out=y_rows[:, :, first * P : last * P], in_=y_f32[first][:])

        def quantize_y(b):
            first, last = [c for c in chunks if c[0] <= b < c[1]][0]
            cols = slice(b * P, (b + 1) * P)
            nc.vector.quantize_mx(out=y_w[:, cols].bitcast(FP8X4), scales=y_s[:, cols], in_=y_bf[b][:].rearrange("p j t -> p (j t)"))
            if b == last - 1:
                nc.sync.dma_start(out=y_words[:, first * P : last * P], in_=y_w[:, first * P : last * P])

        def vector_round(u):
            if u < len(units):
                subtract(u)
            done = u - 2
            if done >= len(units) - 2 and done < len(units):
                quantize_z(len(units) - 2, done % 2, 1)
            elif 0 <= done < len(units) and done % 2 == 1:
                quantize_z(done - 1, 0, 2)
            if 0 <= u - 1 < len(units):
                weigh(u - 1)
            if 0 <= u - 5 < len(units) and units[u - 5][1] == GROUPS - 1:
                quantize_y(units[u - 5][0])
            if 0 <= u - 4 < len(units) and units[u - 4][1] == GROUPS - 1:
                finish(units[u - 4][0])

        gather_words("b", 0)
        gather_scales("b", 0)
        gather_scales("a", 0)
        deal_w8(1)
        round_w1(0)
        quantize_w1(0)
        later_w = keep.tile([P, 3, HALF], U16, name="later_w", tag="later_w", align_bytes=64)
        for i, key in enumerate([("a", 0), ("b", 1), ("a", 1)]):
            picked_w[key] = later_w[:, i, :]
        gather_words("a", 0)
        deal_w8(2)

        def prepare(s):
            if s in (1, 3):
                round_w1(1 + s // 3)
            if s in (2, 3):
                quantize_w1(s - 1)
            if s in (4, 5):
                side = "b" if s == 4 else "a"
                gather_words(side, 1)
                gather_scales(side, 1)
            if s == 6:
                deal_w4()

        square_step(0)
        for s in range(len(steps)):
            if s + 1 < len(steps):
                square_step(s + 1)
            log_step(s)
            for side, u in steps[s]:
                if side == "a":
                    vector_round(u)
            prepare(s)
        for u in range(len(units), len(units) + 5):
            vector_round(u)
        for q in range(4):
            queue = nc.scalar if q % 2 else nc.sync
            queue.dma_start(out=out_2[0, 4 * q : 4 * q + 4, :].bitcast(I32), in_=y_s[32 * q : 32 * q + 4, :].bitcast(I32))
